import numpy as np
import ml_dtypes


def mxq(x, axis, fmt="e4m3"):
    dtype, down = {"e4m3": (ml_dtypes.float8_e4m3fn, 7), "e5m2": (ml_dtypes.float8_e5m2, 14)}[fmt]
    v = np.moveaxis(np.asarray(x, np.float32).astype(ml_dtypes.bfloat16).astype(np.float64), axis, -1)
    blocks = v.reshape(v.shape[:-1] + (-1, 32))
    amax = np.abs(blocks).max(-1, keepdims=True)
    byte = np.maximum(np.where(amax > 0, np.frexp(amax)[1] - 1 + 127, 0) - down, 1)
    scale = np.exp2(byte - 127.0)
    codes = (blocks / scale).astype(np.float32).astype(dtype).astype(np.float64)
    return np.moveaxis((codes * scale).reshape(v.shape), -1, axis)


WIDE = False


def mx_kscale(k):
    if not WIDE:
        return np.ones(k)
    levels = np.array([10, -10, 5, -5, 0])
    if k % 512:
        return np.exp2(np.random.permutation(np.resize(levels, k // 32))).repeat(32)
    a = np.empty((k // 512, 16))
    for p in range(k // 512):
        a[p, :8] = np.random.permutation(np.resize(levels, 8))
        for g in range(8):
            far = levels[np.abs(levels - a[p, g]) >= 10]
            a[p, g + 8] = far[np.random.randint(len(far))]
    return np.exp2(a.ravel()).repeat(32)


def f64(x):
    return np.asarray(x).astype(np.float64)


def striped(idx):
    return np.tile(idx.reshape(-1, 16).T, (8, 1)).astype(np.uint16)


def unstriped(offs):
    return offs[:16].T.reshape(-1).astype(np.int64)


E2M1 = np.array([0.0, 0.5, 1.0, 1.5, 2.0, 3.0, 4.0, 6.0, -0.0, -0.5, -1.0, -1.5, -2.0, -3.0, -4.0, -6.0])


def pack_weight(w, fmt):
    k, n = w.shape
    w = f64(np.asarray(w, np.float32).astype(ml_dtypes.bfloat16)).reshape(k // 32, 32, n)
    amax = np.abs(w).max(1)
    if fmt == "e4m3":
        byte = np.frexp(amax)[1] - 1 + 127 - 7
    else:
        mant, ex = np.frexp(amax / 6.0)
        byte = np.where(mant > 0.5, ex, ex - 1) + 127
    byte = np.clip(np.where(amax > 0, byte, 1), 1, 254)
    scaled = (w * np.exp2(127.0 - byte)[:, None, :]).reshape(k, n).astype(np.float32)
    by_word = np.ascontiguousarray(scaled.reshape(k // 512, 128, 4, n).transpose(0, 1, 3, 2))
    if fmt == "e4m3":
        words = by_word.astype(ml_dtypes.float8_e4m3fn).view(np.uint8)
    else:
        c = by_word.astype(ml_dtypes.float4_e2m1fn).view(np.uint8) & 0xF
        words = (c[..., 0::2] | (c[..., 1::2] << 4)).reshape(k // 512, 128, 2 * n)
    return np.ascontiguousarray(words), np.ascontiguousarray(byte.astype(np.uint8).reshape(k // 512, 16, n))


def unpack_weight(words, scales, fmt):
    g, _, n = scales.shape
    words = np.ascontiguousarray(words).reshape(g, 128, n, -1)
    if fmt == "e4m3":
        vals = words.view(ml_dtypes.float8_e4m3fn).astype(np.float64)
    else:
        nib = np.empty((g, 128, n, 4), np.uint8)
        nib[..., 0::2] = words & 0xF
        nib[..., 1::2] = words >> 4
        vals = E2M1[nib]
    vals = vals * np.repeat(np.exp2(scales.astype(np.float64) - 127.0), 8, axis=1)[..., None]
    return vals.transpose(0, 1, 3, 2).reshape(g * 512, n)


def gelu(v):
    return 0.5 * v * (1.0 + np.tanh(np.sqrt(2.0 / np.pi) * (v + 0.044715 * v**3)))


K, T, S, H, S2, T3, P = 512, 4096, 1024, 1024, 512, 2048, 512

def setup_inputs():
    n = np.random.standard_normal
    s = mx_kscale(K)[:, None]
    u = mx_kscale(H)[:, None]
    tab_words, tab_scales = pack_weight(n((K, T)) * s, "e4m3")
    tab2_words, tab2_scales = pack_weight(n((H, T3)) / u / np.sqrt(H), "e4m3")
    w2_words, w2_scales = pack_weight(n((K, H)) / s * u.T / np.sqrt(K), "e2m1")
    return {
        "tab_words": tab_words, "tab_scales": tab_scales,
        "tab2_words": tab2_words, "tab2_scales": tab2_scales,
        "offs": striped(np.random.permutation(T)[:S]),
        "offs2": striped(np.random.permutation(T3)[:S2]),
        "pos1": striped(np.random.permutation(S)[:P]),
        "pos2": striped(np.random.permutation(S)[:P]),
        "w1": (n((K, H)) / s / np.sqrt(K)).astype(np.float32),
        "b1": (0.5 * n(H)).astype(np.float32),
        "gain": (np.random.uniform(0.7, 1.5, H) * u[:, 0]).astype(np.float32),
        "w2_words": w2_words, "w2_scales": w2_scales,
        "w5": (0.5 * n((H, S2)) / u / np.sqrt(H)).astype(np.float32),
        "sc": np.random.uniform(0.6, 3.0, S2).astype(np.float32),
        "th": n(S2).astype(np.float32),
        "lift": (np.sign(n(S2)) * np.random.uniform(0.6, 1.8, S2)).astype(np.float32),
    }

def reference(tab_words, tab_scales, tab2_words, tab2_scales, offs, offs2, pos1, pos2,
              w1, b1, gain, w2_words, w2_scales, w5, sc, th, lift):
    v = unpack_weight(tab_words, tab_scales, "e4m3")[:, unstriped(offs)]
    v2 = unpack_weight(tab2_words, tab2_scales, "e4m3")[:, unstriped(offs2)]
    w2 = unpack_weight(w2_words, w2_scales, "e2m1")
    z = (mxq(f64(w1), 0, "e4m3").T @ v) + f64(b1)[:, None]
    h = f64(gain)[:, None] * (z / (1.0 + np.exp(-z)))
    f = w2.T @ v
    hq = mxq(h, 0, "e4m3")
    fq = mxq(f, 0, "e4m3")
    e = v2.T @ hq + mxq(f64(w5), 0, "e4m3").T @ fq
    a = 1.0 / (1.0 + np.exp(-(f64(sc)[:, None] * e[:, unstriped(pos1)] + f64(th)[:, None])))
    return np.minimum(f64(lift)[:, None] * a, e[:, unstriped(pos2)])

@@ -1,0 +1,262 @@
+from contextlib import ExitStack
+
+import concourse.mybir as mybir
+
+K, T, S, H, S2, T3, NP = 512, 4096, 1024, 1024, 512, 2048, 512
+FLOPS = 2 * (2 * K * H * S + 2 * H * S2 * S)
+
+F32 = mybir.dt.float32
+BF16 = mybir.dt.bfloat16
+I32 = mybir.dt.int32
+U32 = mybir.dt.uint32
+U16 = mybir.dt.uint16
+U8 = mybir.dt.uint8
+FP8X4 = mybir.dt.float8_e4m3fn_x4
+FP4X4 = mybir.dt.float4_e2m1fn_x4
+ACT = mybir.ActivationFunctionType
+ALU = mybir.AluOpType
+
+P = 128
+PACK = 4
+PASS = P * PACK
+BANK = 512
+R_PASSES = H // PASS
+HALVES = S // BANK
+M_TILES = S2 // P
+QUADS = 4
+COLS = BANK // 16
+
+
+def tile_list_board_seat_shortlist_kernel(
+    tc, tab_words, tab_scales, tab2_words, tab2_scales, offs, offs2, pos1, pos2,
+    w1, b1, gain, w2_words, w2_scales, w5, sc, th, lift, out,
+):
+    nc = tc.nc
+    with ExitStack() as ctx:
+        keep = ctx.enter_context(tc.tile_pool(name="keep", bufs=1))
+        ring = ctx.enter_context(tc.tile_pool(name="ring", bufs=2))
+        first_psum = ctx.enter_context(tc.psum_pool(name="first_psum", bufs=4))
+        score_psum = ctx.enter_context(tc.psum_pool(name="score_psum", bufs=4))
+
+        def held(name, shape, dtype):
+            return keep.tile(shape, dtype, name=name, align_bytes=64)
+
+        def operand(name, width):
+            return held(name + "_codes", [P, width], U32), held(name + "_scales", [P, width], U8)
+
+        def quantise(dst, grouped):
+            nc.vector.quantize_mx(out=dst[0][:].bitcast(FP8X4), scales=dst[1][:], in_=grouped[:])
+
+        offs_t = held("offs_t", [P, S // 16], U16)
+        offs2_t = held("offs2_t", [P, S2 // 16], U16)
+        pos1_t = held("pos1_t", [P, NP // 16], U16)
+        pos2_t = held("pos2_t", [P, NP // 16], U16)
+        tab_w = held("tab_w", [P, T], U32)
+        tab_s = held("tab_s", [P, T], U8)
+        tab2_w = [held("tab2_w%d" % b, [P, T3], U32) for b in range(R_PASSES)]
+        tab2_s = held("tab2_s", [P, T3], U8)
+        w2_w = held("w2_w", [P, 2 * H], U8)
+        w2_s = held("w2_s", [P, H], U8)
+        w1_raw = [held("w1_raw%d" % b, [P, PACK, PASS], F32) for b in range(R_PASSES)]
+        w5_raw = [held("w5_raw%d" % b, [P, PACK, S2], F32) for b in range(R_PASSES)]
+        b1_t = held("b1_t", [P, R_PASSES, PACK], F32)
+        gain_t = held("gain_t", [P, R_PASSES, PACK], F32)
+        sc_t = held("sc_t", [P, M_TILES], F32)
+        th_t = held("th_t", [P, M_TILES], F32)
+        lift_t = held("lift_t", [P, M_TILES], F32)
+
+        for plane in (w2_s, tab_s, tab2_s):
+            nc.vector.memset(plane[:].bitcast(I32), 0)
+
+        nc.sync.dma_start(offs_t[:], offs)
+        nc.sync.dma_start(w2_w[:].bitcast(I32), w2_words[0].bitcast(I32))
+        for q in range(QUADS):
+            nc.sync.dma_start(w2_s[32 * q : 32 * q + 4, :].bitcast(I32), w2_scales[0, 4 * q : 4 * q + 4, :].bitcast(I32))
+        nc.sync.dma_start(tab_w[:].bitcast(I32), tab_words[0].rearrange("p t i -> p (t i)").bitcast(I32))
+        for q in range(QUADS):
+            nc.sync.dma_start(tab_s[32 * q : 32 * q + 4, :].bitcast(I32), tab_scales[0, 4 * q : 4 * q + 4, :].bitcast(I32))
+        w1_rows = w1.rearrange("(p j) c -> p j c", j=PACK)
+        nc.sync.dma_start(w1_raw[0][:], w1_rows[:, :, 0:PASS])
+        nc.sync.dma_start(b1_t[:], b1.rearrange("(b p t) -> p b t", b=R_PASSES, t=PACK))
+        nc.sync.dma_start(gain_t[:], gain.rearrange("(b p t) -> p b t", b=R_PASSES, t=PACK))
+        nc.sync.dma_start(w1_raw[1][:], w1_rows[:, :, PASS : 2 * PASS])
+        nc.sync.dma_start(offs2_t[:], offs2)
+        for b in range(R_PASSES):
+            nc.sync.dma_start(tab2_w[b][:].bitcast(I32), tab2_words[b].rearrange("p t i -> p (t i)").bitcast(I32))
+        for q in range(QUADS):
+            nc.sync.dma_start(tab2_s[32 * q : 32 * q + 8, :].bitcast(I32), tab2_scales[:, 4 * q : 4 * q + 4, :].bitcast(I32))
+        for b in range(R_PASSES):
+            nc.sync.dma_start(w5_raw[b][:], w5[b * PASS : (b + 1) * PASS, :].rearrange("(p j) m -> p j m", j=PACK))
+        nc.sync.dma_start(pos1_t[:], pos1)
+        nc.sync.dma_start(pos2_t[:], pos2)
+        with nc.allow_non_contiguous_dma(reason="one value a row of scores, on that row's partition"):
+            for dst, vec in ((sc_t, sc), (th_t, th), (lift_t, lift)):
+                nc.sync.dma_start(dst[:], vec.rearrange("(m p) -> p m", p=P))
+
+        w2_dw = held("w2_dw", [P, 2 * H], U8)
+        w2_ds = held("w2_ds", [P, H], U8)
+        nc.vector.tensor_copy(
+            out=w2_dw[:].rearrange("p (b t m e) -> p b m t e", b=R_PASSES, t=PACK, e=2),
+            in_=w2_w[:].rearrange("p (b m t e) -> p b m t e", b=R_PASSES, t=PACK, e=2),
+        )
+        nc.vector.tensor_copy(
+            out=w2_ds[:].rearrange("p (b t m) -> p b t m", b=R_PASSES, t=PACK),
+            in_=w2_s[:].rearrange("p (b m t) -> p b t m", b=R_PASSES, t=PACK),
+        )
+
+        v = [operand("v%d" % jh, BANK) for jh in range(HALVES)]
+        v2_w = [held("v2_w%d" % b, [P, S2], U32) for b in range(R_PASSES)]
+        v2_s = held("v2_s", [P, S2], U8)
+        w1_q = [operand("w1q%d" % b, PASS) for b in range(R_PASSES)]
+        w5_q = [operand("w5q%d" % b, S2) for b in range(R_PASSES)]
+        h_q = {}
+        f_q = {}
+        for b in range(R_PASSES):
+            for jh in range(HALVES):
+                h_q[b, jh] = operand("hq%d%d" % (b, jh), BANK)
+                f_q[b, jh] = operand("fq%d%d" % (b, jh), BANK)
+        scores = [held("scores%d" % mt, [P, S], F32) for mt in range(M_TILES)]
+
+        def gather_v(jh):
+            part = offs_t[:, jh * COLS : (jh + 1) * COLS]
+            nc.vector.tensor_copy(v[jh][0][:], tab_w[:].indirect(part))
+            nc.vector.tensor_copy(v[jh][1][:], tab_s[:].indirect(part))
+
+        def gather_v2():
+            for b in range(R_PASSES):
+                nc.vector.tensor_copy(v2_w[b][:], tab2_w[b][:].indirect(offs2_t[:]))
+            nc.vector.tensor_copy(v2_s[:], tab2_s[:].indirect(offs2_t[:]))
+
+        def round_w1(b, copy):
+            grouped = ring.tile([P, PACK * PASS], BF16, name="w_grouped", align_bytes=64)
+            copy(
+                out=grouped[:].rearrange("p (t m j) -> p m j t", t=PACK, j=PACK),
+                in_=w1_raw[b][:].rearrange("p j (m t) -> p m j t", t=PACK),
+            )
+            return grouped
+
+        def round_w5(b):
+            grouped = ring.tile([P, PACK * S2], BF16, name="w_grouped", align_bytes=64)
+            nc.vector.tensor_copy(
+                out=grouped[:].rearrange("p (c i j) -> p c j i", i=2, j=PACK),
+                in_=w5_raw[b][:].rearrange("p j (c i) -> p c j i", i=2),
+            )
+            return grouped
+
+        def plain_branch(b, jh):
+            grouped = ring.tile([P, PACK * BANK], BF16, name="f_grouped", align_bytes=64)
+            for g in range(BANK // P):
+                cols = slice(g * P, (g + 1) * P)
+                bank = first_psum.tile([P, PACK, P], F32, name="bank")
+                for t in range(PACK):
+                    c0 = (b * PACK + t) * P
+                    nc.tensor.matmul_mx(
+                        out=bank[:, t, :],
+                        lhsT=w2_dw[:, 2 * c0 : 2 * (c0 + P)].bitcast(FP4X4),
+                        lhsT_scale=w2_ds[:, c0 : c0 + P],
+                        rhs=v[jh][0][:, cols].bitcast(FP8X4),
+                        rhs_scale=v[jh][1][:, cols],
+                        start=True,
+                        stop=True,
+                    )
+                nc.scalar.copy(
+                    out=grouped[:, g * BANK : (g + 1) * BANK].rearrange("p (n t) -> p n t", t=PACK),
+                    in_=bank[:].rearrange("p t n -> p n t"),
+                )
+            return grouped
+
+        def bent_branch(b, jh):
+            bent = ring.tile([P, PACK, BANK], F32, name="bent", align_bytes=64)
+            for t in range(PACK):
+                cols = slice(t * P, (t + 1) * P)
+                bank = first_psum.tile([P, BANK], F32, name="bank")
+                nc.tensor.matmul_mx(
+                    out=bank[:],
+                    lhsT=w1_q[b][0][:, cols].bitcast(FP8X4),
+                    lhsT_scale=w1_q[b][1][:, cols],
+                    rhs=v[jh][0][:].bitcast(FP8X4),
+                    rhs_scale=v[jh][1][:],
+                    start=True,
+                    stop=True,
+                )
+                nc.scalar.activation(out=bent[:, t, :], in_=bank[:], func=ACT.Silu, bias=b1_t[:, b, t : t + 1])
+            return bent
+
+        def apply_gain(b, bent):
+            grouped = ring.tile([P, PACK * BANK], BF16, name="h_grouped", align_bytes=64)
+            nc.vector.tensor_tensor(
+                out=grouped[:].rearrange("p (c i t) -> p c t i", i=2, t=PACK),
+                in0=bent[:].rearrange("p t (c i) -> p c t i", i=2),
+                in1=gain_t[:, b, :].unsqueeze(1).unsqueeze(3).to_broadcast([P, BANK // 2, PACK, 2]),
+                op=ALU.mult,
+            )
+            return grouped
+
+        def score_pass(bank, mt, jh, kind, b, start, stop):
+            cols = slice(mt * P, (mt + 1) * P)
+            if kind == "h":
+                lhs, lhs_scale, rhs = v2_w[b][:, cols], v2_s[4 * b : P, cols], h_q[b, jh]
+            else:
+                lhs, lhs_scale, rhs = w5_q[b][0][:, cols], w5_q[b][1][:, cols], f_q[b, jh]
+            nc.tensor.matmul_mx(
+                out=bank[:], lhsT=lhs.bitcast(FP8X4), lhsT_scale=lhs_scale,
+                rhs=rhs[0][:].bitcast(FP8X4), rhs_scale=rhs[1][:], start=start, stop=stop,
+            )
+
+        def score_banks(jh, order):
+            banks = [score_psum.tile([P, BANK], F32, name="score_bank") for mt in range(M_TILES)]
+            for n, (kind, b) in enumerate(order):
+                for mt in range(M_TILES):
+                    score_pass(banks[mt], mt, jh, kind, b, n == 0, n == len(order) - 1)
+            return banks
+
+        gather_v(0)
+        g = round_w1(0, nc.scalar.copy)
+        f00 = plain_branch(0, 0)
+        gather_v(1)
+        quantise(w1_q[0], g)
+        g = round_w1(1, nc.vector.tensor_copy)
+        z00 = bent_branch(0, 0)
+        quantise(f_q[0, 0], f00)
+        quantise(w1_q[1], g)
+        f10 = plain_branch(1, 0)
+        h00 = apply_gain(0, z00)
+        gather_v2()
+        quantise(h_q[0, 0], h00)
+        z10 = bent_branch(1, 0)
+        quantise(f_q[1, 0], f10)
+        g0 = round_w5(0)
+        z01 = bent_branch(0, 1)
+        h10 = apply_gain(1, z10)
+        quantise(w5_q[0], g0)
+        g1 = round_w5(1)
+        quantise(h_q[1, 0], h10)
+        z11 = bent_branch(1, 1)
+        quantise(w5_q[1], g1)
+        h01 = apply_gain(0, z01)
+        banks0 = score_banks(0, [("f", 0), ("h", 0), ("h", 1), ("f", 1)])
+        f01 = plain_branch(0, 1)
+        h11 = apply_gain(1, z11)
+        quantise(h_q[0, 1], h01)
+        for mt in range(M_TILES):
+            nc.scalar.copy(out=scores[mt][:, 0:BANK], in_=banks0[mt][:])
+        quantise(f_q[0, 1], f01)
+        quantise(h_q[1, 1], h11)
+        f11 = plain_branch(1, 1)
+        quantise(f_q[1, 1], f11)
+        banks1 = score_banks(1, [("h", 0), ("f", 0), ("h", 1), ("f", 1)])
+        for mt in range(M_TILES):
+            copy = nc.vector.tensor_copy if mt == 0 else nc.scalar.copy
+            copy(out=scores[mt][:, BANK:S], in_=banks1[mt][:])
+            look = ring.tile([P, NP], F32, name="look", align_bytes=64)
+            nc.scalar.activation(
+                out=look[:], in_=scores[mt][:].indirect(pos1_t[:]), func=ACT.Sigmoid,
+                bias=th_t[:, mt : mt + 1], scale=sc_t[:, mt : mt + 1],
+            )
+            plain = ring.tile([P, NP], F32, name="plain", align_bytes=64)
+            nc.vector.tensor_copy(plain[:], scores[mt][:].indirect(pos2_t[:]))
+            result = ring.tile([P, NP], F32, name="result", align_bytes=64)
+            nc.vector.scalar_tensor_tensor(
+                out=result[:], in0=look[:], scalar=lift_t[:, mt : mt + 1], in1=plain[:], op0=ALU.mult, op1=ALU.min,
+            )
+            nc.sync.dma_start(out[mt * P : (mt + 1) * P, :], result[:])

@@ -24,6 +24,7 @@ R_PASSES = H // PASS
 HALVES = S // BANK
 M_TILES = S2 // P
 QUADS = 4
+PART = BANK // 2
 COLS = BANK // 16
 
 
@@ -34,9 +35,11 @@ def tile_list_board_seat_shortlist_kernel(
     nc = tc.nc
     with ExitStack() as ctx:
         keep = ctx.enter_context(tc.tile_pool(name="keep", bufs=1))
-        ring = ctx.enter_context(tc.tile_pool(name="ring", bufs=2))
-        first_psum = ctx.enter_context(tc.psum_pool(name="first_psum", bufs=4))
-        score_psum = ctx.enter_context(tc.psum_pool(name="score_psum", bufs=4))
+        ring = ctx.enter_context(tc.tile_pool(name="ring", bufs=4))
+        psum = ctx.enter_context(tc.psum_pool(name="psum", bufs=1))
+
+        def take_bank(index, shape):
+            return psum.tile(shape, F32, name="bank%d" % index)
 
         def held(name, shape, dtype):
             return keep.tile(shape, dtype, name=name, align_bytes=64)
@@ -65,26 +68,35 @@ def tile_list_board_seat_shortlist_kernel(
         th_t = held("th_t", [P, M_TILES], F32)
         lift_t = held("lift_t", [P, M_TILES], F32)
 
-        for plane in (w2_s, tab_s, tab2_s):
-            nc.vector.memset(plane[:].bitcast(I32), 0)
+        nc.vector.memset(tab_s[:, 0 : T // 2].bitcast(I32), 0)
+        nc.gpsimd.memset(tab_s[:, T // 2 : T].bitcast(I32), 0)
+        nc.vector.memset(w2_s[:].bitcast(I32), 0)
+        nc.vector.memset(tab2_s[:].bitcast(I32), 0)
+
+        tab_rows = tab_words[0].rearrange("p t i -> p (t i)").bitcast(I32)
+
+        def load_tab(lo, hi):
+            nc.sync.dma_start(tab_w[:, lo:hi].bitcast(I32), tab_rows[:, lo:hi])
 
         nc.sync.dma_start(offs_t[:], offs)
         nc.sync.dma_start(w2_w[:].bitcast(I32), w2_words[0].bitcast(I32))
-        for q in range(QUADS):
-            nc.sync.dma_start(w2_s[32 * q : 32 * q + 4, :].bitcast(I32), w2_scales[0, 4 * q : 4 * q + 4, :].bitcast(I32))
-        nc.sync.dma_start(tab_w[:].bitcast(I32), tab_words[0].rearrange("p t i -> p (t i)").bitcast(I32))
+        load_tab(0, T // 4)
+        load_tab(T // 4, T // 2)
+        nc.sync.dma_start(b1_t[:], b1.rearrange("(b p t) -> p b t", b=R_PASSES, t=PACK))
         for q in range(QUADS):
             nc.sync.dma_start(tab_s[32 * q : 32 * q + 4, :].bitcast(I32), tab_scales[0, 4 * q : 4 * q + 4, :].bitcast(I32))
+        load_tab(T // 2, T)
+        for q in range(QUADS):
+            nc.sync.dma_start(w2_s[32 * q : 32 * q + 4, :].bitcast(I32), w2_scales[0, 4 * q : 4 * q + 4, :].bitcast(I32))
         w1_rows = w1.rearrange("(p j) c -> p j c", j=PACK)
         nc.sync.dma_start(w1_raw[0][:], w1_rows[:, :, 0:PASS])
-        nc.sync.dma_start(b1_t[:], b1.rearrange("(b p t) -> p b t", b=R_PASSES, t=PACK))
-        nc.sync.dma_start(gain_t[:], gain.rearrange("(b p t) -> p b t", b=R_PASSES, t=PACK))
-        nc.sync.dma_start(w1_raw[1][:], w1_rows[:, :, PASS : 2 * PASS])
         nc.sync.dma_start(offs2_t[:], offs2)
-        for b in range(R_PASSES):
-            nc.sync.dma_start(tab2_w[b][:].bitcast(I32), tab2_words[b].rearrange("p t i -> p (t i)").bitcast(I32))
         for q in range(QUADS):
             nc.sync.dma_start(tab2_s[32 * q : 32 * q + 8, :].bitcast(I32), tab2_scales[:, 4 * q : 4 * q + 4, :].bitcast(I32))
+        nc.sync.dma_start(w1_raw[1][:], w1_rows[:, :, PASS : 2 * PASS])
+        nc.sync.dma_start(gain_t[:], gain.rearrange("(b p t) -> p b t", b=R_PASSES, t=PACK))
+        for b in range(R_PASSES):
+            nc.sync.dma_start(tab2_w[b][:].bitcast(I32), tab2_words[b].rearrange("p t i -> p (t i)").bitcast(I32))
         for b in range(R_PASSES):
             nc.sync.dma_start(w5_raw[b][:], w5[b * PASS : (b + 1) * PASS, :].rearrange("(p j) m -> p j m", j=PACK))
         nc.sync.dma_start(pos1_t[:], pos1)
@@ -93,11 +105,15 @@ def tile_list_board_seat_shortlist_kernel(
             for dst, vec in ((sc_t, sc), (th_t, th), (lift_t, lift)):
                 nc.sync.dma_start(dst[:], vec.rearrange("(m p) -> p m", p=P))
 
+        zero = held("zero", [P, 1], F32)
+        nc.vector.memset(zero[:], 0.0)
+        warm = held("warm", [P, 2], F32)
+        nc.scalar.activation(out=warm[:, 0:1], in_=zero[:], func=ACT.Silu)
         w2_dw = held("w2_dw", [P, 2 * H], U8)
         w2_ds = held("w2_ds", [P, H], U8)
         nc.vector.tensor_copy(
-            out=w2_dw[:].rearrange("p (b t m e) -> p b m t e", b=R_PASSES, t=PACK, e=2),
-            in_=w2_w[:].rearrange("p (b m t e) -> p b m t e", b=R_PASSES, t=PACK, e=2),
+            out=w2_dw[:].bitcast(U16).rearrange("p (b t m) -> p b m t", b=R_PASSES, t=PACK),
+            in_=w2_w[:].bitcast(U16).rearrange("p (b m t) -> p b m t", b=R_PASSES, t=PACK),
         )
         nc.vector.tensor_copy(
             out=w2_ds[:].rearrange("p (b t m) -> p b t m", b=R_PASSES, t=PACK),
@@ -135,19 +151,19 @@ def tile_list_board_seat_shortlist_kernel(
             )
             return grouped
 
-        def round_w5(b):
+        def round_w5(b, copy):
             grouped = ring.tile([P, PACK * S2], BF16, name="w_grouped", align_bytes=64)
-            nc.vector.tensor_copy(
+            copy(
                 out=grouped[:].rearrange("p (c i j) -> p c j i", i=2, j=PACK),
                 in_=w5_raw[b][:].rearrange("p j (c i) -> p c j i", i=2),
             )
             return grouped
 
-        def plain_branch(b, jh):
+        def plain_branch(b, jh, bank0):
             grouped = ring.tile([P, PACK * BANK], BF16, name="f_grouped", align_bytes=64)
             for g in range(BANK // P):
                 cols = slice(g * P, (g + 1) * P)
-                bank = first_psum.tile([P, PACK, P], F32, name="bank")
+                bank = take_bank(bank0 + g, [P, PACK, P])
                 for t in range(PACK):
                     c0 = (b * PACK + t) * P
                     nc.tensor.matmul_mx(
@@ -169,7 +185,7 @@ def tile_list_board_seat_shortlist_kernel(
             bent = ring.tile([P, PACK, BANK], F32, name="bent", align_bytes=64)
             for t in range(PACK):
                 cols = slice(t * P, (t + 1) * P)
-                bank = first_psum.tile([P, BANK], F32, name="bank")
+                bank = take_bank(t, [P, BANK])
                 nc.tensor.matmul_mx(
                     out=bank[:],
                     lhsT=w1_q[b][0][:, cols].bitcast(FP8X4),
@@ -182,72 +198,92 @@ def tile_list_board_seat_shortlist_kernel(
                 nc.scalar.activation(out=bent[:, t, :], in_=bank[:], func=ACT.Silu, bias=b1_t[:, b, t : t + 1])
             return bent
 
-        def apply_gain(b, bent):
-            grouped = ring.tile([P, PACK * BANK], BF16, name="h_grouped", align_bytes=64)
+        def apply_gain(b, bent, grouped, part):
+            cols = slice(part * PART, (part + 1) * PART)
             nc.vector.tensor_tensor(
-                out=grouped[:].rearrange("p (c i t) -> p c t i", i=2, t=PACK),
-                in0=bent[:].rearrange("p t (c i) -> p c t i", i=2),
-                in1=gain_t[:, b, :].unsqueeze(1).unsqueeze(3).to_broadcast([P, BANK // 2, PACK, 2]),
+                out=grouped[:, PACK * cols.start : PACK * cols.stop].rearrange("p (c i t) -> p c t i", i=2, t=PACK),
+                in0=bent[:, :, cols].rearrange("p t (c i) -> p c t i", i=2),
+                in1=gain_t[:, b, :].unsqueeze(1).unsqueeze(3).to_broadcast([P, PART // 2, PACK, 2]),
                 op=ALU.mult,
             )
-            return grouped
 
-        def score_pass(bank, mt, jh, kind, b, start, stop):
-            cols = slice(mt * P, (mt + 1) * P)
-            if kind == "h":
-                lhs, lhs_scale, rhs = v2_w[b][:, cols], v2_s[4 * b : P, cols], h_q[b, jh]
-            else:
-                lhs, lhs_scale, rhs = w5_q[b][0][:, cols], w5_q[b][1][:, cols], f_q[b, jh]
-            nc.tensor.matmul_mx(
-                out=bank[:], lhsT=lhs.bitcast(FP8X4), lhsT_scale=lhs_scale,
-                rhs=rhs[0][:].bitcast(FP8X4), rhs_scale=rhs[1][:], start=start, stop=stop,
+        def quantise_part(dst, grouped, part):
+            cols = slice(part * PART, (part + 1) * PART)
+            nc.vector.quantize_mx(
+                out=dst[0][:, cols].bitcast(FP8X4), scales=dst[1][:, cols],
+                in_=grouped[:, PACK * cols.start : PACK * cols.stop],
             )
 
-        def score_banks(jh, order):
-            banks = [score_psum.tile([P, BANK], F32, name="score_bank") for mt in range(M_TILES)]
-            for n, (kind, b) in enumerate(order):
+        def score_pass(bank, mt, jh, kind, b, cols, start, stop):
+            rows = slice(mt * P, (mt + 1) * P)
+            if kind == "h":
+                lhs, lhs_scale, rhs = v2_w[b][:, rows], v2_s[4 * b : P, rows], h_q[b, jh]
+            else:
+                lhs, lhs_scale, rhs = w5_q[b][0][:, rows], w5_q[b][1][:, rows], f_q[b, jh]
+            nc.tensor.matmul_mx(
+                out=bank[:, cols], lhsT=lhs.bitcast(FP8X4), lhsT_scale=lhs_scale,
+                rhs=rhs[0][:, cols].bitcast(FP8X4), rhs_scale=rhs[1][:, cols], start=start, stop=stop,
+            )
+
+        def score_banks(jh, bank0, early, late):
+            banks = [take_bank(bank0 + mt, [P, BANK]) for mt in range(M_TILES)]
+            for n, (kind, b, cols) in enumerate(early):
                 for mt in range(M_TILES):
-                    score_pass(banks[mt], mt, jh, kind, b, n == 0, n == len(order) - 1)
+                    score_pass(banks[mt], mt, jh, kind, b, cols, n == 0, False)
+            for mt in range(M_TILES):
+                for n, (kind, b, cols) in enumerate(late):
+                    score_pass(banks[mt], mt, jh, kind, b, cols, False, n == len(late) - 1)
             return banks
 
+        last_bent = []
+
+        def bent_chunk(b, jh):
+            bent = bent_branch(b, jh)
+            last_bent.append(bent)
+            grouped = ring.tile([P, PACK * BANK], BF16, name="h_grouped", align_bytes=64)
+            for part in range(BANK // PART):
+                apply_gain(b, bent, grouped, part)
+            return grouped
+
         gather_v(0)
-        g = round_w1(0, nc.scalar.copy)
-        f00 = plain_branch(0, 0)
+        f00 = plain_branch(0, 0, 0)
         gather_v(1)
+        g = round_w1(0, nc.vector.tensor_copy)
+        f10 = plain_branch(1, 0, 4)
         quantise(w1_q[0], g)
         g = round_w1(1, nc.vector.tensor_copy)
-        z00 = bent_branch(0, 0)
         quantise(f_q[0, 0], f00)
         quantise(w1_q[1], g)
-        f10 = plain_branch(1, 0)
-        h00 = apply_gain(0, z00)
+        quantise(f_q[1, 0], f10)
+        h00 = bent_chunk(0, 0)
+        f01 = plain_branch(0, 1, 4)
+        f11 = plain_branch(1, 1, 4)
         gather_v2()
         quantise(h_q[0, 0], h00)
-        z10 = bent_branch(1, 0)
-        quantise(f_q[1, 0], f10)
-        g0 = round_w5(0)
-        z01 = bent_branch(0, 1)
-        h10 = apply_gain(1, z10)
+        g0 = round_w5(0, nc.vector.tensor_copy)
+        quantise(f_q[0, 1], f01)
+        g1 = round_w5(1, nc.vector.tensor_copy)
         quantise(w5_q[0], g0)
-        g1 = round_w5(1)
-        quantise(h_q[1, 0], h10)
-        z11 = bent_branch(1, 1)
+        quantise(f_q[1, 1], f11)
         quantise(w5_q[1], g1)
-        h01 = apply_gain(0, z01)
-        banks0 = score_banks(0, [("f", 0), ("h", 0), ("h", 1), ("f", 1)])
-        f01 = plain_branch(0, 1)
-        h11 = apply_gain(1, z11)
+        h10 = bent_chunk(1, 0)
+        quantise(h_q[1, 0], h10)
+        h01 = bent_chunk(0, 1)
         quantise(h_q[0, 1], h01)
+        h11 = bent_chunk(1, 1)
+        nc.scalar.activation(out=warm[:, 1:2], in_=last_bent[-1][:, PACK - 1, 0:1], func=ACT.Sigmoid)
+        for part in range(BANK // PART):
+            quantise_part(h_q[1, 1], h11, part)
+        whole = slice(0, BANK)
+        early = [("f", 0, whole), ("f", 1, whole), ("h", 0, whole)]
+        banks0 = score_banks(0, 4, [("h", 0, whole), ("f", 0, whole), ("f", 1, whole)], [("h", 1, whole)])
         for mt in range(M_TILES):
             nc.scalar.copy(out=scores[mt][:, 0:BANK], in_=banks0[mt][:])
-        quantise(f_q[0, 1], f01)
-        quantise(h_q[1, 1], h11)
-        f11 = plain_branch(1, 1)
-        quantise(f_q[1, 1], f11)
-        banks1 = score_banks(1, [("h", 0), ("f", 0), ("h", 1), ("f", 1)])
+        banks1 = score_banks(1, 0, early, [("h", 1, slice(0, PART)), ("h", 1, slice(PART, BANK))])
         for mt in range(M_TILES):
             copy = nc.vector.tensor_copy if mt == 0 else nc.scalar.copy
             copy(out=scores[mt][:, BANK:S], in_=banks1[mt][:])
+        for mt in range(M_TILES):
             look = ring.tile([P, NP], F32, name="look", align_bytes=64)
             nc.scalar.activation(
                 out=look[:], in_=scores[mt][:].indirect(pos1_t[:]), func=ACT.Sigmoid,

@@ -62,8 +62,8 @@ def tile_list_board_seat_shortlist_kernel(
         w2_s = held("w2_s", [P, H], U8)
         w1_raw = [held("w1_raw%d" % b, [P, PACK, PASS], F32) for b in range(R_PASSES)]
         w5_raw = [held("w5_raw%d" % b, [P, PACK, S2], F32) for b in range(R_PASSES)]
-        b1_t = held("b1_t", [P, R_PASSES, PACK], F32)
-        gain_t = held("gain_t", [P, R_PASSES, PACK], F32)
+        b1_t = held("b1_t", [P, R_PASSES, 2 * PACK], F32)
+        gain_t = held("gain_t", [P, R_PASSES, 2 * PACK], F32)
         sc_t = held("sc_t", [P, M_TILES], F32)
         th_t = held("th_t", [P, M_TILES], F32)
         lift_t = held("lift_t", [P, M_TILES], F32)
@@ -82,23 +82,23 @@ def tile_list_board_seat_shortlist_kernel(
         nc.sync.dma_start(w2_w[:].bitcast(I32), w2_words[0].bitcast(I32))
         load_tab(0, T // 4)
         load_tab(T // 4, T // 2)
-        nc.sync.dma_start(b1_t[:], b1.rearrange("(b p t) -> p b t", b=R_PASSES, t=PACK))
-        for q in range(QUADS):
-            nc.sync.dma_start(tab_s[32 * q : 32 * q + 4, :].bitcast(I32), tab_scales[0, 4 * q : 4 * q + 4, :].bitcast(I32))
+        nc.sync.dma_start(offs2_t[:], offs2)
+        for r in range(4):
+            nc.sync.dma_start(tab_s[r:P:32, :].bitcast(I32), tab_scales[0, r:16:4, :].bitcast(I32))
         load_tab(T // 2, T)
-        for q in range(QUADS):
-            nc.sync.dma_start(w2_s[32 * q : 32 * q + 4, :].bitcast(I32), w2_scales[0, 4 * q : 4 * q + 4, :].bitcast(I32))
+        for r in range(4):
+            nc.sync.dma_start(w2_s[r:P:32, :].bitcast(I32), w2_scales[0, r:16:4, :].bitcast(I32))
         w1_rows = w1.rearrange("(p j) c -> p j c", j=PACK)
         nc.sync.dma_start(w1_raw[0][:], w1_rows[:, :, 0:PASS])
-        nc.sync.dma_start(offs2_t[:], offs2)
+        nc.sync.dma_start(b1_t[:, :, 0:PACK], b1.rearrange("(b p t) -> p b t", b=R_PASSES, t=PACK))
         for q in range(QUADS):
             nc.sync.dma_start(tab2_s[32 * q : 32 * q + 8, :].bitcast(I32), tab2_scales[:, 4 * q : 4 * q + 4, :].bitcast(I32))
         nc.sync.dma_start(w1_raw[1][:], w1_rows[:, :, PASS : 2 * PASS])
-        nc.sync.dma_start(gain_t[:], gain.rearrange("(b p t) -> p b t", b=R_PASSES, t=PACK))
-        for b in range(R_PASSES):
-            nc.sync.dma_start(tab2_w[b][:].bitcast(I32), tab2_words[b].rearrange("p t i -> p (t i)").bitcast(I32))
+        nc.sync.dma_start(gain_t[:, :, 0:PACK], gain.rearrange("(b p t) -> p b t", b=R_PASSES, t=PACK))
         for b in range(R_PASSES):
             nc.sync.dma_start(w5_raw[b][:], w5[b * PASS : (b + 1) * PASS, :].rearrange("(p j) m -> p j m", j=PACK))
+        for b in range(R_PASSES):
+            nc.sync.dma_start(tab2_w[b][:].bitcast(I32), tab2_words[b].rearrange("p t i -> p (t i)").bitcast(I32))
         nc.sync.dma_start(pos1_t[:], pos1)
         nc.sync.dma_start(pos2_t[:], pos2)
         with nc.allow_non_contiguous_dma(reason="one value a row of scores, on that row's partition"):
@@ -181,11 +181,11 @@ def tile_list_board_seat_shortlist_kernel(
                 )
             return grouped
 
-        def bent_branch(b, jh):
+        def bent_branch(b, jh, bank0):
             bent = ring.tile([P, PACK, BANK], F32, name="bent", align_bytes=64)
             for t in range(PACK):
                 cols = slice(t * P, (t + 1) * P)
-                bank = take_bank(t, [P, BANK])
+                bank = take_bank(bank0 + t, [P, BANK])
                 nc.tensor.matmul_mx(
                     out=bank[:],
                     lhsT=w1_q[b][0][:, cols].bitcast(FP8X4),
@@ -203,7 +203,7 @@ def tile_list_board_seat_shortlist_kernel(
             nc.vector.tensor_tensor(
                 out=grouped[:, PACK * cols.start : PACK * cols.stop].rearrange("p (c i t) -> p c t i", i=2, t=PACK),
                 in0=bent[:, :, cols].rearrange("p t (c i) -> p c t i", i=2),
-                in1=gain_t[:, b, :].unsqueeze(1).unsqueeze(3).to_broadcast([P, PART // 2, PACK, 2]),
+                in1=gain_t[:, b, 0:PACK].unsqueeze(1).unsqueeze(3).to_broadcast([P, PART // 2, PACK, 2]),
                 op=ALU.mult,
             )
 
@@ -235,15 +235,16 @@ def tile_list_board_seat_shortlist_kernel(
                     score_pass(banks[mt], mt, jh, kind, b, cols, False, n == len(late) - 1)
             return banks
 
-        last_bent = []
-
-        def bent_chunk(b, jh):
-            bent = bent_branch(b, jh)
-            last_bent.append(bent)
+        def bent_chunk(b, jh, bank0):
+            bent = bent_branch(b, jh, bank0)
             grouped = ring.tile([P, PACK * BANK], BF16, name="h_grouped", align_bytes=64)
             for part in range(BANK // PART):
                 apply_gain(b, bent, grouped, part)
-            return grouped
+            return bent, grouped
+
+        def quantise_parts(dst, grouped):
+            for part in range(BANK // PART):
+                quantise_part(dst, grouped, part)
 
         gather_v(0)
         f00 = plain_branch(0, 0, 0)
@@ -255,33 +256,32 @@ def tile_list_board_seat_shortlist_kernel(
         quantise(f_q[0, 0], f00)
         quantise(w1_q[1], g)
         quantise(f_q[1, 0], f10)
-        h00 = bent_chunk(0, 0)
+        z, h00 = bent_chunk(0, 0, 0)
         f01 = plain_branch(0, 1, 4)
         f11 = plain_branch(1, 1, 4)
-        gather_v2()
         quantise(h_q[0, 0], h00)
         g0 = round_w5(0, nc.vector.tensor_copy)
         quantise(f_q[0, 1], f01)
         g1 = round_w5(1, nc.vector.tensor_copy)
         quantise(w5_q[0], g0)
         quantise(f_q[1, 1], f11)
+        gather_v2()
         quantise(w5_q[1], g1)
-        h10 = bent_chunk(1, 0)
-        quantise(h_q[1, 0], h10)
-        h01 = bent_chunk(0, 1)
-        quantise(h_q[0, 1], h01)
-        h11 = bent_chunk(1, 1)
-        nc.scalar.activation(out=warm[:, 1:2], in_=last_bent[-1][:, PACK - 1, 0:1], func=ACT.Sigmoid)
-        for part in range(BANK // PART):
-            quantise_part(h_q[1, 1], h11, part)
-        whole = slice(0, BANK)
-        early = [("f", 0, whole), ("f", 1, whole), ("h", 0, whole)]
-        banks0 = score_banks(0, 4, [("h", 0, whole), ("f", 0, whole), ("f", 1, whole)], [("h", 1, whole)])
+        z, h10 = bent_chunk(1, 0, 0)
+        quantise_parts(h_q[1, 0], h10)
+        z, h01 = bent_chunk(0, 1, 4)
+        quantise_parts(h_q[0, 1], h01)
+        z, h11 = bent_chunk(1, 1, 0)
+        nc.scalar.activation(out=warm[:, 1:2], in_=z[:, PACK - 1, 0:1], func=ACT.Sigmoid)
+        quantise_parts(h_q[1, 1], h11)
+        whole, left, right = slice(0, BANK), slice(0, PART), slice(PART, BANK)
+        banks0 = score_banks(0, 4, [("f", 0, whole), ("f", 1, whole), ("h", 0, whole)], [("h", 1, left), ("h", 1, right)])
         for mt in range(M_TILES):
-            nc.scalar.copy(out=scores[mt][:, 0:BANK], in_=banks0[mt][:])
-        banks1 = score_banks(1, 0, early, [("h", 1, slice(0, PART)), ("h", 1, slice(PART, BANK))])
+            copy = nc.vector.tensor_copy if mt < 0 else nc.scalar.copy
+            copy(out=scores[mt][:, 0:BANK], in_=banks0[mt][:])
+        banks1 = score_banks(1, 0, [("f", 0, whole), ("f", 1, whole), ("h", 0, left), ("h", 0, right)], [("h", 1, left), ("h", 1, right)])
         for mt in range(M_TILES):
-            copy = nc.vector.tensor_copy if mt == 0 else nc.scalar.copy
+            copy = nc.vector.tensor_copy if mt < 1 else nc.scalar.copy
             copy(out=scores[mt][:, BANK:S], in_=banks1[mt][:])
         for mt in range(M_TILES):
             look = ring.tile([P, NP], F32, name="look", align_bytes=64)

@@ -2,7 +2,7 @@ from contextlib import ExitStack
 
 import concourse.mybir as mybir
 
-K, T, S, H, S2, T3, NP = 512, 4096, 1024, 1024, 512, 2048, 512
+K, T, S, H, S2, T3, PICKS = 512, 4096, 1024, 1024, 512, 2048, 512
 FLOPS = 2 * (2 * K * H * S + 2 * H * S2 * S)
 
 F32 = mybir.dt.float32
@@ -20,12 +20,16 @@ P = 128
 PACK = 4
 PASS = P * PACK
 BANK = 512
+PART = BANK // 2
+LIST_COLUMN = 16
+QUADRANT = 32
+SCALE_ROWS = 4
 R_PASSES = H // PASS
 HALVES = S // BANK
 M_TILES = S2 // P
-QUADS = 4
-PART = BANK // 2
-COLS = BANK // 16
+LOW_BANKS, HIGH_BANKS = 0, 4
+CHUNKS = R_PASSES * HALVES
+VECTOR_EMPTIES = 2
 
 
 def tile_list_board_seat_shortlist_kernel(
@@ -35,7 +39,7 @@ def tile_list_board_seat_shortlist_kernel(
     nc = tc.nc
     with ExitStack() as ctx:
         keep = ctx.enter_context(tc.tile_pool(name="keep", bufs=1))
-        ring = ctx.enter_context(tc.tile_pool(name="ring", bufs=4))
+        stage = ctx.enter_context(tc.tile_pool(name="stage", bufs=CHUNKS))
         psum = ctx.enter_context(tc.psum_pool(name="psum", bufs=1))
 
         def take_bank(index, shape):
@@ -44,16 +48,16 @@ def tile_list_board_seat_shortlist_kernel(
         def held(name, shape, dtype):
             return keep.tile(shape, dtype, name=name, align_bytes=64)
 
+        def staged(name, shape, dtype, bufs=CHUNKS):
+            return stage.tile(shape, dtype, name=name, align_bytes=64, bufs=bufs)
+
         def operand(name, width):
             return held(name + "_codes", [P, width], U32), held(name + "_scales", [P, width], U8)
 
-        def quantise(dst, grouped):
-            nc.vector.quantize_mx(out=dst[0][:].bitcast(FP8X4), scales=dst[1][:], in_=grouped[:])
-
-        offs_t = held("offs_t", [P, S // 16], U16)
-        offs2_t = held("offs2_t", [P, S2 // 16], U16)
-        pos1_t = held("pos1_t", [P, NP // 16], U16)
-        pos2_t = held("pos2_t", [P, NP // 16], U16)
+        offs_t = held("offs_t", [P, S // LIST_COLUMN], U16)
+        offs2_t = held("offs2_t", [P, S2 // LIST_COLUMN], U16)
+        pos1_t = held("pos1_t", [P, PICKS // LIST_COLUMN], U16)
+        pos2_t = held("pos2_t", [P, PICKS // LIST_COLUMN], U16)
         tab_w = held("tab_w", [P, T], U32)
         tab_s = held("tab_s", [P, T], U8)
         tab2_w = [held("tab2_w%d" % b, [P, T3], U32) for b in range(R_PASSES)]
@@ -78,30 +82,38 @@ def tile_list_board_seat_shortlist_kernel(
         def load_tab(lo, hi):
             nc.sync.dma_start(tab_w[:, lo:hi].bitcast(I32), tab_rows[:, lo:hi])
 
+        def load_plane(plane, rows):
+            for r in range(SCALE_ROWS):
+                nc.sync.dma_start(plane[r:P:QUADRANT, :].bitcast(I32), rows[r :: SCALE_ROWS, :].bitcast(I32))
+
+        def load_by_r(dst, vec):
+            nc.sync.dma_start(dst[:, :, 0:PACK], vec.rearrange("(b p t) -> p b t", b=R_PASSES, t=PACK))
+
         nc.sync.dma_start(offs_t[:], offs)
         nc.sync.dma_start(w2_w[:].bitcast(I32), w2_words[0].bitcast(I32))
         load_tab(0, T // 4)
         load_tab(T // 4, T // 2)
         nc.sync.dma_start(offs2_t[:], offs2)
-        for r in range(4):
-            nc.sync.dma_start(tab_s[r:P:32, :].bitcast(I32), tab_scales[0, r:16:4, :].bitcast(I32))
+        load_plane(tab_s, tab_scales[0])
         load_tab(T // 2, T)
-        for r in range(4):
-            nc.sync.dma_start(w2_s[r:P:32, :].bitcast(I32), w2_scales[0, r:16:4, :].bitcast(I32))
+        load_plane(w2_s, w2_scales[0])
         w1_rows = w1.rearrange("(p j) c -> p j c", j=PACK)
         nc.sync.dma_start(w1_raw[0][:], w1_rows[:, :, 0:PASS])
-        nc.sync.dma_start(b1_t[:, :, 0:PACK], b1.rearrange("(b p t) -> p b t", b=R_PASSES, t=PACK))
-        for q in range(QUADS):
-            nc.sync.dma_start(tab2_s[32 * q : 32 * q + 8, :].bitcast(I32), tab2_scales[:, 4 * q : 4 * q + 4, :].bitcast(I32))
+        load_by_r(b1_t, b1)
+        for q in range(P // QUADRANT):
+            nc.sync.dma_start(
+                tab2_s[QUADRANT * q : QUADRANT * q + R_PASSES * SCALE_ROWS, :].bitcast(I32),
+                tab2_scales[:, SCALE_ROWS * q : SCALE_ROWS * (q + 1), :].bitcast(I32),
+            )
         nc.sync.dma_start(w1_raw[1][:], w1_rows[:, :, PASS : 2 * PASS])
-        nc.sync.dma_start(gain_t[:, :, 0:PACK], gain.rearrange("(b p t) -> p b t", b=R_PASSES, t=PACK))
+        load_by_r(gain_t, gain)
         for b in range(R_PASSES):
             nc.sync.dma_start(w5_raw[b][:], w5[b * PASS : (b + 1) * PASS, :].rearrange("(p j) m -> p j m", j=PACK))
         for b in range(R_PASSES):
             nc.sync.dma_start(tab2_w[b][:].bitcast(I32), tab2_words[b].rearrange("p t i -> p (t i)").bitcast(I32))
         nc.sync.dma_start(pos1_t[:], pos1)
         nc.sync.dma_start(pos2_t[:], pos2)
-        with nc.allow_non_contiguous_dma(reason="one value a row of scores, on that row's partition"):
+        with nc.allow_non_contiguous_dma(reason="one value a director, on that director's partition"):
             for dst, vec in ((sc_t, sc), (th_t, th), (lift_t, lift)):
                 nc.sync.dma_start(dst[:], vec.rearrange("(m p) -> p m", p=P))
 
@@ -109,18 +121,19 @@ def tile_list_board_seat_shortlist_kernel(
         nc.vector.memset(zero[:], 0.0)
         warm = held("warm", [P, 2], F32)
         nc.scalar.activation(out=warm[:, 0:1], in_=zero[:], func=ACT.Silu)
-        w2_dw = held("w2_dw", [P, 2 * H], U8)
-        w2_ds = held("w2_ds", [P, H], U8)
+
+        w2_dealt_w = held("w2_dealt_w", [P, 2 * H], U8)
+        w2_dealt_s = held("w2_dealt_s", [P, H], U8)
         nc.vector.tensor_copy(
-            out=w2_dw[:].bitcast(U16).rearrange("p (b t m) -> p b m t", b=R_PASSES, t=PACK),
+            out=w2_dealt_w[:].bitcast(U16).rearrange("p (b t m) -> p b m t", b=R_PASSES, t=PACK),
             in_=w2_w[:].bitcast(U16).rearrange("p (b m t) -> p b m t", b=R_PASSES, t=PACK),
         )
         nc.vector.tensor_copy(
-            out=w2_ds[:].rearrange("p (b t m) -> p b t m", b=R_PASSES, t=PACK),
+            out=w2_dealt_s[:].rearrange("p (b t m) -> p b t m", b=R_PASSES, t=PACK),
             in_=w2_s[:].rearrange("p (b m t) -> p b t m", b=R_PASSES, t=PACK),
         )
 
-        v = [operand("v%d" % jh, BANK) for jh in range(HALVES)]
+        v = [operand("v%d" % half, BANK) for half in range(HALVES)]
         v2_w = [held("v2_w%d" % b, [P, S2], U32) for b in range(R_PASSES)]
         v2_s = held("v2_s", [P, S2], U8)
         w1_q = [operand("w1q%d" % b, PASS) for b in range(R_PASSES)]
@@ -128,50 +141,57 @@ def tile_list_board_seat_shortlist_kernel(
         h_q = {}
         f_q = {}
         for b in range(R_PASSES):
-            for jh in range(HALVES):
-                h_q[b, jh] = operand("hq%d%d" % (b, jh), BANK)
-                f_q[b, jh] = operand("fq%d%d" % (b, jh), BANK)
+            for half in range(HALVES):
+                h_q[b, half] = operand("hq%d%d" % (b, half), BANK)
+                f_q[b, half] = operand("fq%d%d" % (b, half), BANK)
         scores = [held("scores%d" % mt, [P, S], F32) for mt in range(M_TILES)]
+        whole, left, right = slice(0, BANK), slice(0, PART), slice(PART, BANK)
 
-        def gather_v(jh):
-            part = offs_t[:, jh * COLS : (jh + 1) * COLS]
-            nc.vector.tensor_copy(v[jh][0][:], tab_w[:].indirect(part))
-            nc.vector.tensor_copy(v[jh][1][:], tab_s[:].indirect(part))
+        def quantise(dst, grouped, cols):
+            nc.vector.quantize_mx(
+                out=dst[0][:, cols].bitcast(FP8X4), scales=dst[1][:, cols],
+                in_=grouped[:, PACK * cols.start : PACK * cols.stop],
+            )
+
+        def gather_v(half):
+            entries = offs_t[:, half * BANK // LIST_COLUMN : (half + 1) * BANK // LIST_COLUMN]
+            nc.vector.tensor_copy(v[half][0][:], tab_w[:].indirect(entries))
+            nc.vector.tensor_copy(v[half][1][:], tab_s[:].indirect(entries))
 
         def gather_v2():
             for b in range(R_PASSES):
                 nc.vector.tensor_copy(v2_w[b][:], tab2_w[b][:].indirect(offs2_t[:]))
             nc.vector.tensor_copy(v2_s[:], tab2_s[:].indirect(offs2_t[:]))
 
-        def round_w1(b, copy):
-            grouped = ring.tile([P, PACK * PASS], BF16, name="w_grouped", align_bytes=64)
-            copy(
+        def round_w1(b):
+            grouped = staged("w_grouped", [P, PACK * PASS], BF16, R_PASSES)
+            nc.vector.tensor_copy(
                 out=grouped[:].rearrange("p (t m j) -> p m j t", t=PACK, j=PACK),
                 in_=w1_raw[b][:].rearrange("p j (m t) -> p m j t", t=PACK),
             )
             return grouped
 
-        def round_w5(b, copy):
-            grouped = ring.tile([P, PACK * S2], BF16, name="w_grouped", align_bytes=64)
-            copy(
+        def round_w5(b):
+            grouped = staged("w_grouped", [P, PACK * S2], BF16, R_PASSES)
+            nc.vector.tensor_copy(
                 out=grouped[:].rearrange("p (c i j) -> p c j i", i=2, j=PACK),
                 in_=w5_raw[b][:].rearrange("p j (c i) -> p c j i", i=2),
             )
             return grouped
 
-        def plain_branch(b, jh, bank0):
-            grouped = ring.tile([P, PACK * BANK], BF16, name="f_grouped", align_bytes=64)
+        def plain_branch(b, half, bank0):
+            grouped = staged("f_grouped", [P, PACK * BANK], BF16)
             for g in range(BANK // P):
                 cols = slice(g * P, (g + 1) * P)
                 bank = take_bank(bank0 + g, [P, PACK, P])
                 for t in range(PACK):
-                    c0 = (b * PACK + t) * P
+                    place = (b * PACK + t) * P
                     nc.tensor.matmul_mx(
                         out=bank[:, t, :],
-                        lhsT=w2_dw[:, 2 * c0 : 2 * (c0 + P)].bitcast(FP4X4),
-                        lhsT_scale=w2_ds[:, c0 : c0 + P],
-                        rhs=v[jh][0][:, cols].bitcast(FP8X4),
-                        rhs_scale=v[jh][1][:, cols],
+                        lhsT=w2_dealt_w[:, 2 * place : 2 * (place + P)].bitcast(FP4X4),
+                        lhsT_scale=w2_dealt_s[:, place : place + P],
+                        rhs=v[half][0][:, cols].bitcast(FP8X4),
+                        rhs_scale=v[half][1][:, cols],
                         start=True,
                         stop=True,
                     )
@@ -181,8 +201,8 @@ def tile_list_board_seat_shortlist_kernel(
                 )
             return grouped
 
-        def bent_branch(b, jh, bank0):
-            bent = ring.tile([P, PACK, BANK], F32, name="bent", align_bytes=64)
+        def silu_branch(b, half, bank0):
+            bent = staged("bent", [P, PACK, BANK], F32)
             for t in range(PACK):
                 cols = slice(t * P, (t + 1) * P)
                 bank = take_bank(bank0 + t, [P, BANK])
@@ -190,16 +210,15 @@ def tile_list_board_seat_shortlist_kernel(
                     out=bank[:],
                     lhsT=w1_q[b][0][:, cols].bitcast(FP8X4),
                     lhsT_scale=w1_q[b][1][:, cols],
-                    rhs=v[jh][0][:].bitcast(FP8X4),
-                    rhs_scale=v[jh][1][:],
+                    rhs=v[half][0][:].bitcast(FP8X4),
+                    rhs_scale=v[half][1][:],
                     start=True,
                     stop=True,
                 )
                 nc.scalar.activation(out=bent[:, t, :], in_=bank[:], func=ACT.Silu, bias=b1_t[:, b, t : t + 1])
             return bent
 
-        def apply_gain(b, bent, grouped, part):
-            cols = slice(part * PART, (part + 1) * PART)
+        def gain_on_vector(b, bent, grouped, cols):
             nc.vector.tensor_tensor(
                 out=grouped[:, PACK * cols.start : PACK * cols.stop].rearrange("p (c i t) -> p c t i", i=2, t=PACK),
                 in0=bent[:, :, cols].rearrange("p t (c i) -> p c t i", i=2),
@@ -207,92 +226,98 @@ def tile_list_board_seat_shortlist_kernel(
                 op=ALU.mult,
             )
 
-        def quantise_part(dst, grouped, part):
-            cols = slice(part * PART, (part + 1) * PART)
-            nc.vector.quantize_mx(
-                out=dst[0][:, cols].bitcast(FP8X4), scales=dst[1][:, cols],
-                in_=grouped[:, PACK * cols.start : PACK * cols.stop],
+        def gain_on_scalar(b, bent, grouped, cols):
+            flat = staged("h_flat", [P, PACK, PART], BF16, R_PASSES)
+            for t in range(PACK):
+                nc.scalar.activation(out=flat[:, t, :], in_=bent[:, t, cols], func=ACT.Copy, scale=gain_t[:, b, t : t + 1])
+            nc.vector.tensor_copy(
+                out=grouped[:, PACK * cols.start : PACK * cols.stop].rearrange("p (c i t) -> p c t i", i=4, t=PACK),
+                in_=flat[:].rearrange("p t (c i) -> p c t i", i=4),
             )
 
-        def score_pass(bank, mt, jh, kind, b, cols, start, stop):
+        def bent_branch(b, half, bank0):
+            bent = silu_branch(b, half, bank0)
+            grouped = staged("h_grouped", [P, PACK * BANK], BF16)
+            gain_on_vector(b, bent, grouped, left)
+            gain_right = gain_on_scalar if half == HALVES - 1 else gain_on_vector
+            gain_right(b, bent, grouped, right)
+            return bent, grouped
+
+        def score_pass(bank, mt, half, kind, b, cols, start, stop):
             rows = slice(mt * P, (mt + 1) * P)
             if kind == "h":
-                lhs, lhs_scale, rhs = v2_w[b][:, rows], v2_s[4 * b : P, rows], h_q[b, jh]
+                lhs, lhs_scale, rhs = v2_w[b][:, rows], v2_s[SCALE_ROWS * b : P, rows], h_q[b, half]
             else:
-                lhs, lhs_scale, rhs = w5_q[b][0][:, rows], w5_q[b][1][:, rows], f_q[b, jh]
+                lhs, lhs_scale, rhs = w5_q[b][0][:, rows], w5_q[b][1][:, rows], f_q[b, half]
             nc.tensor.matmul_mx(
                 out=bank[:, cols], lhsT=lhs.bitcast(FP8X4), lhsT_scale=lhs_scale,
                 rhs=rhs[0][:, cols].bitcast(FP8X4), rhs_scale=rhs[1][:, cols], start=start, stop=stop,
             )
 
-        def score_banks(jh, bank0, early, late):
+        def score_banks(half, bank0, early):
             banks = [take_bank(bank0 + mt, [P, BANK]) for mt in range(M_TILES)]
             for n, (kind, b, cols) in enumerate(early):
                 for mt in range(M_TILES):
-                    score_pass(banks[mt], mt, jh, kind, b, cols, n == 0, False)
+                    score_pass(banks[mt], mt, half, kind, b, cols, n == 0, False)
             for mt in range(M_TILES):
-                for n, (kind, b, cols) in enumerate(late):
-                    score_pass(banks[mt], mt, jh, kind, b, cols, False, n == len(late) - 1)
+                score_pass(banks[mt], mt, half, "h", 1, left, False, False)
+                score_pass(banks[mt], mt, half, "h", 1, right, False, True)
             return banks
 
-        def bent_chunk(b, jh, bank0):
-            bent = bent_branch(b, jh, bank0)
-            grouped = ring.tile([P, PACK * BANK], BF16, name="h_grouped", align_bytes=64)
-            for part in range(BANK // PART):
-                apply_gain(b, bent, grouped, part)
-            return bent, grouped
-
-        def quantise_parts(dst, grouped):
-            for part in range(BANK // PART):
-                quantise_part(dst, grouped, part)
-
         gather_v(0)
-        f00 = plain_branch(0, 0, 0)
+        f00 = plain_branch(0, 0, LOW_BANKS)
         gather_v(1)
-        g = round_w1(0, nc.vector.tensor_copy)
-        f10 = plain_branch(1, 0, 4)
-        quantise(w1_q[0], g)
-        g = round_w1(1, nc.vector.tensor_copy)
-        quantise(f_q[0, 0], f00)
-        quantise(w1_q[1], g)
-        quantise(f_q[1, 0], f10)
-        z, h00 = bent_chunk(0, 0, 0)
-        f01 = plain_branch(0, 1, 4)
-        f11 = plain_branch(1, 1, 4)
-        quantise(h_q[0, 0], h00)
-        g0 = round_w5(0, nc.vector.tensor_copy)
-        quantise(f_q[0, 1], f01)
-        g1 = round_w5(1, nc.vector.tensor_copy)
-        quantise(w5_q[0], g0)
-        quantise(f_q[1, 1], f11)
+        w1_first = round_w1(0)
+        f10 = plain_branch(1, 0, HIGH_BANKS)
+        quantise(w1_q[0], w1_first, whole)
+        w1_second = round_w1(1)
+        quantise(f_q[0, 0], f00, whole)
+        quantise(w1_q[1], w1_second, whole)
+        quantise(f_q[1, 0], f10, whole)
+        h00 = bent_branch(0, 0, LOW_BANKS)[1]
+        f01 = plain_branch(0, 1, HIGH_BANKS)
+        f11 = plain_branch(1, 1, HIGH_BANKS)
+        quantise(h_q[0, 0], h00, whole)
+        w5_first = round_w5(0)
+        quantise(f_q[0, 1], f01, whole)
+        w5_second = round_w5(1)
+        quantise(w5_q[0], w5_first, whole)
+        quantise(f_q[1, 1], f11, whole)
         gather_v2()
-        quantise(w5_q[1], g1)
-        z, h10 = bent_chunk(1, 0, 0)
-        quantise_parts(h_q[1, 0], h10)
-        z, h01 = bent_chunk(0, 1, 4)
-        quantise_parts(h_q[0, 1], h01)
-        z, h11 = bent_chunk(1, 1, 0)
-        nc.scalar.activation(out=warm[:, 1:2], in_=z[:, PACK - 1, 0:1], func=ACT.Sigmoid)
-        quantise_parts(h_q[1, 1], h11)
-        whole, left, right = slice(0, BANK), slice(0, PART), slice(PART, BANK)
-        banks0 = score_banks(0, 4, [("f", 0, whole), ("f", 1, whole), ("h", 0, whole)], [("h", 1, left), ("h", 1, right)])
+        quantise(w5_q[1], w5_second, whole)
+        for b, half, bank0 in ((1, 0, LOW_BANKS), (0, 1, HIGH_BANKS), (1, 1, LOW_BANKS)):
+            bent, grouped = bent_branch(b, half, bank0)
+            if (b, half) == (R_PASSES - 1, HALVES - 1):
+                nc.scalar.activation(out=warm[:, 1:2], in_=bent[:, PACK - 1, 0:1], func=ACT.Sigmoid)
+            for cols in (left, right):
+                quantise(h_q[b, half], grouped, cols)
+
+        banks = score_banks(0, HIGH_BANKS, [("f", 0, whole), ("f", 1, whole), ("h", 0, whole)])
         for mt in range(M_TILES):
-            copy = nc.vector.tensor_copy if mt < 0 else nc.scalar.copy
-            copy(out=scores[mt][:, 0:BANK], in_=banks0[mt][:])
-        banks1 = score_banks(1, 0, [("f", 0, whole), ("f", 1, whole), ("h", 0, left), ("h", 0, right)], [("h", 1, left), ("h", 1, right)])
+            nc.scalar.copy(out=scores[mt][:, 0:BANK], in_=banks[mt][:])
+        banks = score_banks(1, LOW_BANKS, [("f", 0, whole), ("f", 1, whole), ("h", 0, left), ("h", 0, right)])
         for mt in range(M_TILES):
-            copy = nc.vector.tensor_copy if mt < 1 else nc.scalar.copy
-            copy(out=scores[mt][:, BANK:S], in_=banks1[mt][:])
+            copy = nc.vector.tensor_copy if mt < VECTOR_EMPTIES else nc.scalar.copy
+            copy(out=scores[mt][:, BANK:S], in_=banks[mt][:])
+
         for mt in range(M_TILES):
-            look = ring.tile([P, NP], F32, name="look", align_bytes=64)
-            nc.scalar.activation(
-                out=look[:], in_=scores[mt][:].indirect(pos1_t[:]), func=ACT.Sigmoid,
-                bias=th_t[:, mt : mt + 1], scale=sc_t[:, mt : mt + 1],
-            )
-            plain = ring.tile([P, NP], F32, name="plain", align_bytes=64)
+            look = staged("look", [P, PICKS], F32)
+            plain = staged("plain", [P, PICKS], F32)
+            result = staged("result", [P, PICKS], F32)
+            pieces = 2 if mt == M_TILES - 1 else 1
+            width = PICKS // pieces
+            for n in range(pieces):
+                cols = slice(n * width, (n + 1) * width)
+                nc.scalar.activation(
+                    out=look[:, cols],
+                    in_=scores[mt][:].indirect(pos1_t[:, cols.start // LIST_COLUMN : cols.stop // LIST_COLUMN]),
+                    func=ACT.Sigmoid, bias=th_t[:, mt : mt + 1], scale=sc_t[:, mt : mt + 1],
+                )
             nc.vector.tensor_copy(plain[:], scores[mt][:].indirect(pos2_t[:]))
-            result = ring.tile([P, NP], F32, name="result", align_bytes=64)
-            nc.vector.scalar_tensor_tensor(
-                out=result[:], in0=look[:], scalar=lift_t[:, mt : mt + 1], in1=plain[:], op0=ALU.mult, op1=ALU.min,
-            )
-            nc.sync.dma_start(out[mt * P : (mt + 1) * P, :], result[:])
+            for n in range(pieces):
+                cols = slice(n * width, (n + 1) * width)
+                nc.vector.scalar_tensor_tensor(
+                    out=result[:, cols], in0=look[:, cols], scalar=lift_t[:, mt : mt + 1], in1=plain[:, cols],
+                    op0=ALU.mult, op1=ALU.min,
+                )
+                nc.sync.dma_start(out[mt * P : (mt + 1) * P, cols], result[:, cols])

from contextlib import ExitStack

import concourse.mybir as mybir

K, T, S, H, S2, T3, PICKS = 512, 4096, 1024, 1024, 512, 2048, 512
FLOPS = 2 * (2 * K * H * S + 2 * H * S2 * S)

F32 = mybir.dt.float32
BF16 = mybir.dt.bfloat16
I32 = mybir.dt.int32
U32 = mybir.dt.uint32
U16 = mybir.dt.uint16
U8 = mybir.dt.uint8
FP8X4 = mybir.dt.float8_e4m3fn_x4
FP4X4 = mybir.dt.float4_e2m1fn_x4
ACT = mybir.ActivationFunctionType
ALU = mybir.AluOpType

P = 128
PACK = 4
PASS = P * PACK
BANK = 512
PART = BANK // 2
LIST_COLUMN = 16
QUADRANT = 32
SCALE_ROWS = 4
R_PASSES = H // PASS
HALVES = S // BANK
M_TILES = S2 // P
LOW_BANKS, HIGH_BANKS = 0, 4
CHUNKS = R_PASSES * HALVES
VECTOR_EMPTIES = 2


def tile_list_board_seat_shortlist_kernel(
    tc, tab_words, tab_scales, tab2_words, tab2_scales, offs, offs2, pos1, pos2,
    w1, b1, gain, w2_words, w2_scales, w5, sc, th, lift, out,
):
    nc = tc.nc
    with ExitStack() as ctx:
        keep = ctx.enter_context(tc.tile_pool(name="keep", bufs=1))
        stage = ctx.enter_context(tc.tile_pool(name="stage", bufs=CHUNKS))
        psum = ctx.enter_context(tc.psum_pool(name="psum", bufs=1))

        def take_bank(index, shape):
            return psum.tile(shape, F32, name="bank%d" % index)

        def held(name, shape, dtype):
            return keep.tile(shape, dtype, name=name, align_bytes=64)

        def staged(name, shape, dtype, bufs=CHUNKS):
            return stage.tile(shape, dtype, name=name, align_bytes=64, bufs=bufs)

        def operand(name, width):
            return held(name + "_codes", [P, width], U32), held(name + "_scales", [P, width], U8)

        offs_t = held("offs_t", [P, S // LIST_COLUMN], U16)
        offs2_t = held("offs2_t", [P, S2 // LIST_COLUMN], U16)
        pos1_t = held("pos1_t", [P, PICKS // LIST_COLUMN], U16)
        pos2_t = held("pos2_t", [P, PICKS // LIST_COLUMN], U16)
        tab_w = held("tab_w", [P, T], U32)
        tab_s = held("tab_s", [P, T], U8)
        tab2_w = [held("tab2_w%d" % b, [P, T3], U32) for b in range(R_PASSES)]
        tab2_s = held("tab2_s", [P, T3], U8)
        w2_w = held("w2_w", [P, 2 * H], U8)
        w2_s = held("w2_s", [P, H], U8)
        w1_raw = [held("w1_raw%d" % b, [P, PACK, PASS], F32) for b in range(R_PASSES)]
        w5_raw = [held("w5_raw%d" % b, [P, PACK, S2], F32) for b in range(R_PASSES)]
        b1_t = held("b1_t", [P, R_PASSES, 2 * PACK], F32)
        gain_t = held("gain_t", [P, R_PASSES, 2 * PACK], F32)
        sc_t = held("sc_t", [P, M_TILES], F32)
        th_t = held("th_t", [P, M_TILES], F32)
        lift_t = held("lift_t", [P, M_TILES], F32)

        nc.vector.memset(tab_s[:, 0 : T // 2].bitcast(I32), 0)
        nc.gpsimd.memset(tab_s[:, T // 2 : T].bitcast(I32), 0)
        nc.vector.memset(w2_s[:].bitcast(I32), 0)
        nc.vector.memset(tab2_s[:].bitcast(I32), 0)

        tab_rows = tab_words[0].rearrange("p t i -> p (t i)").bitcast(I32)

        def load_tab(lo, hi):
            nc.sync.dma_start(tab_w[:, lo:hi].bitcast(I32), tab_rows[:, lo:hi])

        def load_plane(plane, rows):
            for r in range(SCALE_ROWS):
                nc.sync.dma_start(plane[r:P:QUADRANT, :].bitcast(I32), rows[r :: SCALE_ROWS, :].bitcast(I32))

        def load_by_r(dst, vec):
            nc.sync.dma_start(dst[:, :, 0:PACK], vec.rearrange("(b p t) -> p b t", b=R_PASSES, t=PACK))

        nc.sync.dma_start(offs_t[:], offs)
        nc.sync.dma_start(w2_w[:].bitcast(I32), w2_words[0].bitcast(I32))
        load_tab(0, T // 4)
        load_tab(T // 4, T // 2)
        nc.sync.dma_start(offs2_t[:], offs2)
        load_plane(tab_s, tab_scales[0])
        load_tab(T // 2, T)
        load_plane(w2_s, w2_scales[0])
        w1_rows = w1.rearrange("(p j) c -> p j c", j=PACK)
        nc.sync.dma_start(w1_raw[0][:], w1_rows[:, :, 0:PASS])
        load_by_r(b1_t, b1)
        for q in range(P // QUADRANT):
            nc.sync.dma_start(
                tab2_s[QUADRANT * q : QUADRANT * q + R_PASSES * SCALE_ROWS, :].bitcast(I32),
                tab2_scales[:, SCALE_ROWS * q : SCALE_ROWS * (q + 1), :].bitcast(I32),
            )
        nc.sync.dma_start(w1_raw[1][:], w1_rows[:, :, PASS : 2 * PASS])
        load_by_r(gain_t, gain)
        for b in range(R_PASSES):
            nc.sync.dma_start(w5_raw[b][:], w5[b * PASS : (b + 1) * PASS, :].rearrange("(p j) m -> p j m", j=PACK))
        for b in range(R_PASSES):
            nc.sync.dma_start(tab2_w[b][:].bitcast(I32), tab2_words[b].rearrange("p t i -> p (t i)").bitcast(I32))
        nc.sync.dma_start(pos1_t[:], pos1)
        nc.sync.dma_start(pos2_t[:], pos2)
        with nc.allow_non_contiguous_dma(reason="one value a director, on that director's partition"):
            for dst, vec in ((sc_t, sc), (th_t, th), (lift_t, lift)):
                nc.sync.dma_start(dst[:], vec.rearrange("(m p) -> p m", p=P))

        zero = held("zero", [P, 1], F32)
        nc.vector.memset(zero[:], 0.0)
        warm = held("warm", [P, 2], F32)
        nc.scalar.activation(out=warm[:, 0:1], in_=zero[:], func=ACT.Silu)

        w2_dealt_w = held("w2_dealt_w", [P, 2 * H], U8)
        w2_dealt_s = held("w2_dealt_s", [P, H], U8)
        nc.vector.tensor_copy(
            out=w2_dealt_w[:].bitcast(U16).rearrange("p (b t m) -> p b m t", b=R_PASSES, t=PACK),
            in_=w2_w[:].bitcast(U16).rearrange("p (b m t) -> p b m t", b=R_PASSES, t=PACK),
        )
        nc.vector.tensor_copy(
            out=w2_dealt_s[:].rearrange("p (b t m) -> p b t m", b=R_PASSES, t=PACK),
            in_=w2_s[:].rearrange("p (b m t) -> p b t m", b=R_PASSES, t=PACK),
        )

        v = [operand("v%d" % half, BANK) for half in range(HALVES)]
        v2_w = [held("v2_w%d" % b, [P, S2], U32) for b in range(R_PASSES)]
        v2_s = held("v2_s", [P, S2], U8)
        w1_q = [operand("w1q%d" % b, PASS) for b in range(R_PASSES)]
        w5_q = [operand("w5q%d" % b, S2) for b in range(R_PASSES)]
        h_q = {}
        f_q = {}
        for b in range(R_PASSES):
            for half in range(HALVES):
                h_q[b, half] = operand("hq%d%d" % (b, half), BANK)
                f_q[b, half] = operand("fq%d%d" % (b, half), BANK)
        scores = [held("scores%d" % mt, [P, S], F32) for mt in range(M_TILES)]
        whole, left, right = slice(0, BANK), slice(0, PART), slice(PART, BANK)

        def quantise(dst, grouped, cols):
            nc.vector.quantize_mx(
                out=dst[0][:, cols].bitcast(FP8X4), scales=dst[1][:, cols],
                in_=grouped[:, PACK * cols.start : PACK * cols.stop],
            )

        def gather_v(half):
            entries = offs_t[:, half * BANK // LIST_COLUMN : (half + 1) * BANK // LIST_COLUMN]
            nc.vector.tensor_copy(v[half][0][:], tab_w[:].indirect(entries))
            nc.vector.tensor_copy(v[half][1][:], tab_s[:].indirect(entries))

        def gather_v2():
            for b in range(R_PASSES):
                nc.vector.tensor_copy(v2_w[b][:], tab2_w[b][:].indirect(offs2_t[:]))
            nc.vector.tensor_copy(v2_s[:], tab2_s[:].indirect(offs2_t[:]))

        def round_w1(b):
            grouped = staged("w_grouped", [P, PACK * PASS], BF16, R_PASSES)
            nc.vector.tensor_copy(
                out=grouped[:].rearrange("p (t m j) -> p m j t", t=PACK, j=PACK),
                in_=w1_raw[b][:].rearrange("p j (m t) -> p m j t", t=PACK),
            )
            return grouped

        def round_w5(b):
            grouped = staged("w_grouped", [P, PACK * S2], BF16, R_PASSES)
            nc.vector.tensor_copy(
                out=grouped[:].rearrange("p (c i j) -> p c j i", i=2, j=PACK),
                in_=w5_raw[b][:].rearrange("p j (c i) -> p c j i", i=2),
            )
            return grouped

        def plain_branch(b, half, bank0):
            grouped = staged("f_grouped", [P, PACK * BANK], BF16)
            for g in range(BANK // P):
                cols = slice(g * P, (g + 1) * P)
                bank = take_bank(bank0 + g, [P, PACK, P])
                for t in range(PACK):
                    place = (b * PACK + t) * P
                    nc.tensor.matmul_mx(
                        out=bank[:, t, :],
                        lhsT=w2_dealt_w[:, 2 * place : 2 * (place + P)].bitcast(FP4X4),
                        lhsT_scale=w2_dealt_s[:, place : place + P],
                        rhs=v[half][0][:, cols].bitcast(FP8X4),
                        rhs_scale=v[half][1][:, cols],
                        start=True,
                        stop=True,
                    )
                nc.scalar.copy(
                    out=grouped[:, g * BANK : (g + 1) * BANK].rearrange("p (n t) -> p n t", t=PACK),
                    in_=bank[:].rearrange("p t n -> p n t"),
                )
            return grouped

        def silu_branch(b, half, bank0):
            bent = staged("bent", [P, PACK, BANK], F32)
            for t in range(PACK):
                cols = slice(t * P, (t + 1) * P)
                bank = take_bank(bank0 + t, [P, BANK])
                nc.tensor.matmul_mx(
                    out=bank[:],
                    lhsT=w1_q[b][0][:, cols].bitcast(FP8X4),
                    lhsT_scale=w1_q[b][1][:, cols],
                    rhs=v[half][0][:].bitcast(FP8X4),
                    rhs_scale=v[half][1][:],
                    start=True,
                    stop=True,
                )
                nc.scalar.activation(out=bent[:, t, :], in_=bank[:], func=ACT.Silu, bias=b1_t[:, b, t : t + 1])
            return bent

        def gain_on_vector(b, bent, grouped, cols):
            nc.vector.tensor_tensor(
                out=grouped[:, PACK * cols.start : PACK * cols.stop].rearrange("p (c i t) -> p c t i", i=2, t=PACK),
                in0=bent[:, :, cols].rearrange("p t (c i) -> p c t i", i=2),
                in1=gain_t[:, b, 0:PACK].unsqueeze(1).unsqueeze(3).to_broadcast([P, PART // 2, PACK, 2]),
                op=ALU.mult,
            )

        def gain_on_scalar(b, bent, grouped, cols):
            flat = staged("h_flat", [P, PACK, PART], BF16, R_PASSES)
            for t in range(PACK):
                nc.scalar.activation(out=flat[:, t, :], in_=bent[:, t, cols], func=ACT.Copy, scale=gain_t[:, b, t : t + 1])
            nc.vector.tensor_copy(
                out=grouped[:, PACK * cols.start : PACK * cols.stop].rearrange("p (c i t) -> p c t i", i=4, t=PACK),
                in_=flat[:].rearrange("p t (c i) -> p c t i", i=4),
            )

        def bent_branch(b, half, bank0):
            bent = silu_branch(b, half, bank0)
            grouped = staged("h_grouped", [P, PACK * BANK], BF16)
            gain_on_vector(b, bent, grouped, left)
            gain_right = gain_on_scalar if half == HALVES - 1 else gain_on_vector
            gain_right(b, bent, grouped, right)
            return bent, grouped

        def score_pass(bank, mt, half, kind, b, cols, start, stop):
            rows = slice(mt * P, (mt + 1) * P)
            if kind == "h":
                lhs, lhs_scale, rhs = v2_w[b][:, rows], v2_s[SCALE_ROWS * b : P, rows], h_q[b, half]
            else:
                lhs, lhs_scale, rhs = w5_q[b][0][:, rows], w5_q[b][1][:, rows], f_q[b, half]
            nc.tensor.matmul_mx(
                out=bank[:, cols], lhsT=lhs.bitcast(FP8X4), lhsT_scale=lhs_scale,
                rhs=rhs[0][:, cols].bitcast(FP8X4), rhs_scale=rhs[1][:, cols], start=start, stop=stop,
            )

        def score_banks(half, bank0, early):
            banks = [take_bank(bank0 + mt, [P, BANK]) for mt in range(M_TILES)]
            for n, (kind, b, cols) in enumerate(early):
                for mt in range(M_TILES):
                    score_pass(banks[mt], mt, half, kind, b, cols, n == 0, False)
            for mt in range(M_TILES):
                score_pass(banks[mt], mt, half, "h", 1, left, False, False)
                score_pass(banks[mt], mt, half, "h", 1, right, False, True)
            return banks

        gather_v(0)
        f00 = plain_branch(0, 0, LOW_BANKS)
        gather_v(1)
        w1_first = round_w1(0)
        f10 = plain_branch(1, 0, HIGH_BANKS)
        quantise(w1_q[0], w1_first, whole)
        w1_second = round_w1(1)
        quantise(f_q[0, 0], f00, whole)
        quantise(w1_q[1], w1_second, whole)
        quantise(f_q[1, 0], f10, whole)
        h00 = bent_branch(0, 0, LOW_BANKS)[1]
        f01 = plain_branch(0, 1, HIGH_BANKS)
        f11 = plain_branch(1, 1, HIGH_BANKS)
        quantise(h_q[0, 0], h00, whole)
        w5_first = round_w5(0)
        quantise(f_q[0, 1], f01, whole)
        w5_second = round_w5(1)
        quantise(w5_q[0], w5_first, whole)
        quantise(f_q[1, 1], f11, whole)
        gather_v2()
        quantise(w5_q[1], w5_second, whole)
        for b, half, bank0 in ((1, 0, LOW_BANKS), (0, 1, HIGH_BANKS), (1, 1, LOW_BANKS)):
            bent, grouped = bent_branch(b, half, bank0)
            if (b, half) == (R_PASSES - 1, HALVES - 1):
                nc.scalar.activation(out=warm[:, 1:2], in_=bent[:, PACK - 1, 0:1], func=ACT.Sigmoid)
            for cols in (left, right):
                quantise(h_q[b, half], grouped, cols)

        banks = score_banks(0, HIGH_BANKS, [("f", 0, whole), ("f", 1, whole), ("h", 0, whole)])
        for mt in range(M_TILES):
            nc.scalar.copy(out=scores[mt][:, 0:BANK], in_=banks[mt][:])
        banks = score_banks(1, LOW_BANKS, [("f", 0, whole), ("f", 1, whole), ("h", 0, left), ("h", 0, right)])
        for mt in range(M_TILES):
            copy = nc.vector.tensor_copy if mt < VECTOR_EMPTIES else nc.scalar.copy
            copy(out=scores[mt][:, BANK:S], in_=banks[mt][:])

        for mt in range(M_TILES):
            look = staged("look", [P, PICKS], F32)
            plain = staged("plain", [P, PICKS], F32)
            result = staged("result", [P, PICKS], F32)
            pieces = 2 if mt == M_TILES - 1 else 1
            width = PICKS // pieces
            for n in range(pieces):
                cols = slice(n * width, (n + 1) * width)
                nc.scalar.activation(
                    out=look[:, cols],
                    in_=scores[mt][:].indirect(pos1_t[:, cols.start // LIST_COLUMN : cols.stop // LIST_COLUMN]),
                    func=ACT.Sigmoid, bias=th_t[:, mt : mt + 1], scale=sc_t[:, mt : mt + 1],
                )
            nc.vector.tensor_copy(plain[:], scores[mt][:].indirect(pos2_t[:]))
            for n in range(pieces):
                cols = slice(n * width, (n + 1) * width)
                nc.vector.scalar_tensor_tensor(
                    out=result[:, cols], in0=look[:, cols], scalar=lift_t[:, mt : mt + 1], in1=plain[:, cols],
                    op0=ALU.mult, op1=ALU.min,
                )
                nc.sync.dma_start(out[mt * P : (mt + 1) * P, cols], result[:, cols])
